import numpy as np
import ml_dtypes


def mxq(x, axis, fmt="e4m3"):
    dtype, down = {"e4m3": (ml_dtypes.float8_e4m3fn, 7), "e5m2": (ml_dtypes.float8_e5m2, 14)}[fmt]
    v = np.moveaxis(np.asarray(x, np.float32).astype(ml_dtypes.bfloat16).astype(np.float64), axis, -1)
    blocks = v.reshape(v.shape[:-1] + (-1, 32))
    amax = np.abs(blocks).max(-1, keepdims=True)
    byte = np.maximum(np.where(amax > 0, np.frexp(amax)[1] - 1 + 127, 0) - down, 1)
    scale = np.exp2(byte - 127.0)
    codes = (blocks / scale).astype(np.float32).astype(dtype).astype(np.float64)
    return np.moveaxis((codes * scale).reshape(v.shape), -1, axis)


WIDE = False


def mx_kscale(k):
    if not WIDE:
        return np.ones(k)
    levels = np.array([10, -10, 5, -5, 0])
    if k % 512:
        return np.exp2(np.random.permutation(np.resize(levels, k // 32))).repeat(32)
    a = np.empty((k // 512, 16))
    for p in range(k // 512):
        a[p, :8] = np.random.permutation(np.resize(levels, 8))
        for g in range(8):
            far = levels[np.abs(levels - a[p, g]) >= 10]
            a[p, g + 8] = far[np.random.randint(len(far))]
    return np.exp2(a.ravel()).repeat(32)


def f64(x):
    return np.asarray(x).astype(np.float64)


E2M1 = np.array([0.0, 0.5, 1.0, 1.5, 2.0, 3.0, 4.0, 6.0, -0.0, -0.5, -1.0, -1.5, -2.0, -3.0, -4.0, -6.0])


def pack_weight(w, fmt):
    k, n = w.shape
    w = f64(np.asarray(w, np.float32).astype(ml_dtypes.bfloat16)).reshape(k // 32, 32, n)
    amax = np.abs(w).max(1)
    if fmt == "e4m3":
        byte = np.frexp(amax)[1] - 1 + 127 - 7
    else:
        mant, ex = np.frexp(amax / 6.0)
        byte = np.where(mant > 0.5, ex, ex - 1) + 127
    byte = np.clip(np.where(amax > 0, byte, 1), 1, 254)
    scaled = (w * np.exp2(127.0 - byte)[:, None, :]).reshape(k, n).astype(np.float32)
    by_word = np.ascontiguousarray(scaled.reshape(k // 512, 128, 4, n).transpose(0, 1, 3, 2))
    if fmt == "e4m3":
        words = by_word.astype(ml_dtypes.float8_e4m3fn).view(np.uint8)
    else:
        c = by_word.astype(ml_dtypes.float4_e2m1fn).view(np.uint8) & 0xF
        words = (c[..., 0::2] | (c[..., 1::2] << 4)).reshape(k // 512, 128, 2 * n)
    return np.ascontiguousarray(words), np.ascontiguousarray(byte.astype(np.uint8).reshape(k // 512, 16, n))


def unpack_weight(words, scales, fmt):
    g, _, n = scales.shape
    words = np.ascontiguousarray(words).reshape(g, 128, n, -1)
    if fmt == "e4m3":
        vals = words.view(ml_dtypes.float8_e4m3fn).astype(np.float64)
    else:
        nib = np.empty((g, 128, n, 4), np.uint8)
        nib[..., 0::2] = words & 0xF
        nib[..., 1::2] = words >> 4
        vals = E2M1[nib]
    vals = vals * np.repeat(np.exp2(scales.astype(np.float64) - 127.0), 8, axis=1)[..., None]
    return vals.transpose(0, 1, 3, 2).reshape(g * 512, n)


def bf(x):
    return np.asarray(x, np.float32).astype(ml_dtypes.bfloat16)


def planes(Y):
    r, m = Y.shape
    b = f64(bf(Y)).reshape(r // 32, 32, m)
    amax = np.abs(b).max(1)
    byte = np.clip(np.where(amax > 0, np.frexp(amax)[1] - 1 + 127 - 7, 1), 1, 254)
    codes = (b * np.exp2(127.0 - byte)[:, None, :]).reshape(r, m).astype(np.float32).astype(ml_dtypes.float8_e4m3fn).view(np.uint8)
    words = codes.reshape(r // 512, 128, 4, m).transpose(0, 1, 3, 2)
    return np.ascontiguousarray(words), np.ascontiguousarray(byte.astype(np.uint8).reshape(r // 512, 16, m))


K, T, R, N = 1024, 512, 512, 512


def setup_inputs():
    n = np.random.standard_normal
    fk = mx_kscale(K)
    fr = mx_kscale(R)
    xtp = pack_weight(n((K, T)) / fk[:, None], "e2m1")
    wap = pack_weight(n((K, R)) * np.random.uniform(0.3, 2.0, (1, R)) / np.sqrt(K) * fk[:, None], "e4m3")
    wbp = pack_weight(n((R, N)) * 1 / np.sqrt(R) / fr[:, None], "e2m1")
    wyp = pack_weight(n((K, N)) * 1 / np.sqrt(K) * fk[:, None], "e4m3")
    return {
        "xt_words": xtp[0],
        "xt_scales": xtp[1],
        "wa_words": wap[0],
        "wa_scales": wap[1],
        "us": (np.random.uniform(0.5, 2.0, (R, 1)) * fr[:, None]).astype(np.float32),
        "wb_words": wbp[0],
        "wb_scales": wbp[1],
        "wy_words": wyp[0],
        "wy_scales": wyp[1],
    }


def reference(xt_words, xt_scales, wa_words, wa_scales, us, wb_words, wb_scales, wy_words, wy_scales):
    xtu = unpack_weight(xt_words, xt_scales, "e2m1")
    wau = unpack_weight(wa_words, wa_scales, "e4m3")
    wbu = unpack_weight(wb_words, wb_scales, "e2m1")
    wyu = unpack_weight(wy_words, wy_scales, "e4m3")
    a = wau.T @ xtu
    hid = a / (np.mean(np.abs(a), axis=1, keepdims=True) + 0.1) * f64(us)
    hidq = mxq(hid, 0, "e4m3")
    y = wbu.T @ hidq + wyu.T @ xtu
    words, scales = planes(y)
    return y, words, scales

@@ -1,0 +1,246 @@
+from contextlib import ExitStack
+
+import concourse.mybir as mybir
+
+K, T, R, N = 1024, 512, 512, 512
+FLOPS = 2 * T * (K * R + R * N + K * N)
+
+F32 = mybir.dt.float32
+BF16 = mybir.dt.bfloat16
+I32 = mybir.dt.int32
+U8 = mybir.dt.uint8
+E4M3 = mybir.dt.float8_e4m3fn_x4
+E2M1 = mybir.dt.float4_e2m1fn_x4
+ALU = mybir.AluOpType
+ACT = mybir.ActivationFunctionType
+
+P = 128
+PACK = 4
+PASSES = K // (P * PACK)
+QUADS = 4
+TQ = 128
+NQ = T // TQ
+RUN = 4
+
+
+def tile_mix_hidden_evened_and_skip_pl_kernel(
+    tc, xt_words, xt_scales, wa_words, wa_scales, us, wb_words, wb_scales, wy_words, wy_scales, out_0, out_1, out_2
+):
+    nc = tc.nc
+    with ExitStack() as ctx:
+        sb = ctx.enter_context(tc.tile_pool(name="sb", bufs=1))
+        ps = ctx.enter_context(tc.psum_pool(name="ps", bufs=1))
+        ctx.enter_context(tc.manual_schedule())
+
+        def sbuf(name, shape, dtype):
+            return sb.tile(shape, dtype, name=name, align_bytes=64)
+
+        x_codes = sbuf("x_codes", [P, PASSES, 2 * T], U8)
+        x_plane = sbuf("x_plane", [P, PASSES, T], U8)
+        wa_raw = sbuf("wa_raw", [P, PASSES, R], I32)
+        wa_plane_raw = sbuf("wa_plane_raw", [P, PASSES, R], U8)
+        wy_raw = sbuf("wy_raw", [P, PASSES, N], I32)
+        wy_plane_raw = sbuf("wy_plane_raw", [P, PASSES, N], U8)
+        wb_raw = sbuf("wb_raw", [P, 2 * N], U8)
+        wb_plane_raw = sbuf("wb_plane_raw", [P, 1, N], U8)
+        us_sb = sbuf("us_sb", [P, PACK], F32)
+        warm = sbuf("warm", [P, 1], F32)
+        warm_out = sbuf("warm_out", [P, 1], F32)
+
+        wa_codes = [[sbuf("wa_codes_%d_%d" % (h, z), [P, 2, P], I32) for z in range(PASSES)] for h in range(2)]
+        wa_plane = sbuf("wa_plane", [P, PASSES, PACK, P], U8)
+        wy_codes = [sbuf("wy_codes_%d" % z, [P, PACK, P], I32) for z in range(PASSES)]
+        wy_plane = sbuf("wy_plane", [P, PASSES, PACK, P], U8)
+        wb_codes = sbuf("wb_codes", [P, PACK, 2 * P], U8)
+        wb_plane = sbuf("wb_plane", [P, 1, PACK, P], U8)
+
+        def load_scale_rows(queue, plane, scales, q):
+            queue.dma_start(
+                out=plane[32 * q : 32 * q + 4, :, :].bitcast(I32),
+                in_=scales[:, 4 * q : 4 * q + 4, :].rearrange("z r c -> r z c").bitcast(I32),
+            )
+
+        def zero(plane):
+            nc.vector.memset(plane[:].rearrange("p z c -> p (z c)").bitcast(I32), 0)
+
+        def deal_plane(dealt, raw):
+            nc.vector.tensor_copy(out=dealt[:], in_=raw[:].rearrange("p z (m j) -> p z j m", j=PACK))
+
+        zero(wa_plane_raw)
+        zero(x_plane)
+        nc.vector.memset(warm[:], 0.0)
+        zero(wy_plane_raw)
+        zero(wb_plane_raw)
+
+        load_scale_rows(nc.scalar, wa_plane_raw, wa_scales, 0)
+        load_scale_rows(nc.scalar, wa_plane_raw, wa_scales, 1)
+        nc.sync.dma_start(out=wa_raw[:], in_=wa_words.rearrange("z p c r -> p z (c r)").bitcast(I32))
+        nc.sync.dma_start(out=x_codes[:].bitcast(I32), in_=xt_words.rearrange("z p c -> p z c").bitcast(I32))
+        load_scale_rows(nc.scalar, wa_plane_raw, wa_scales, 2)
+        load_scale_rows(nc.scalar, wa_plane_raw, wa_scales, 3)
+        load_scale_rows(nc.sync, x_plane, xt_scales, 0)
+        load_scale_rows(nc.sync, x_plane, xt_scales, 1)
+        nc.scalar.activation(out=warm_out[:], in_=warm[:], func=ACT.Abs)
+        load_scale_rows(nc.scalar, x_plane, xt_scales, 2)
+        load_scale_rows(nc.scalar, x_plane, xt_scales, 3)
+        nc.sync.dma_start(out=wy_raw[:], in_=wy_words.rearrange("z p c r -> p z (c r)").bitcast(I32))
+        nc.sync.dma_start(out=wb_raw[:].bitcast(I32), in_=wb_words[0].bitcast(I32))
+        load_scale_rows(nc.scalar, wy_plane_raw, wy_scales, 0)
+        load_scale_rows(nc.scalar, wy_plane_raw, wy_scales, 1)
+        load_scale_rows(nc.sync, wy_plane_raw, wy_scales, 2)
+        load_scale_rows(nc.sync, wy_plane_raw, wy_scales, 3)
+        nc.scalar.dma_start(out=us_sb[:], in_=us.rearrange("(p j) o -> p (j o)", j=PACK))
+        for q in range(QUADS):
+            load_scale_rows(nc.sync, wb_plane_raw, wb_scales, q)
+
+        deal_plane(wa_plane, wa_plane_raw)
+        for h in range(2):
+            for z in range(PASSES):
+                nc.vector.tensor_copy(
+                    out=wa_codes[h][z][:].rearrange("p j m -> p m j"),
+                    in_=wa_raw[:, z, :].rearrange("p (m j) -> p m j", j=PACK)[:, :, 2 * h : 2 * h + 2],
+                )
+        a_ps = [ps.tile([P, T], F32, name="a_ps_%d" % j) for j in range(PACK)]
+        for j in range(PACK):
+            for z in range(PASSES):
+                nc.tensor.matmul_mx(
+                    out=a_ps[j][:],
+                    lhsT=wa_codes[j // 2][z][:, j % 2, :].bitcast(E4M3),
+                    lhsT_scale=wa_plane[:, z, j, :],
+                    rhs=x_codes[:, z, :].bitcast(E2M1),
+                    rhs_scale=x_plane[:, z, :],
+                    start=(z == 0),
+                    stop=(z == PASSES - 1),
+                )
+
+        abs_a = [sbuf("abs_a_%d" % j, [P, T], BF16) for j in range(PACK)]
+        mean = [sbuf("mean_%d" % j, [P, 1], F32) for j in range(PACK)]
+        denom = [sbuf("denom_%d" % j, [P, 1], F32) for j in range(PACK)]
+        inv = [sbuf("inv_%d" % j, [P, 1], F32) for j in range(PACK)]
+        gain = [sbuf("gain_%d" % j, [P, 1], F32) for j in range(PACK)]
+        hid_rows = sbuf("hid_rows", [P, PACK, T], BF16)
+
+        def mean_abs(j):
+            nc.scalar.activation(out=abs_a[j][:], in_=a_ps[j][:], func=ACT.Abs, scale=1.0 / T, accum_out=mean[j][:])
+
+        def add_tenth(j):
+            nc.vector.tensor_scalar(out=denom[j][:], in0=mean[j][:], scalar1=0.1, scalar2=None, op0=ALU.add)
+
+        def invert(j):
+            nc.vector.reciprocal(out=inv[j][:], in_=denom[j][:])
+
+        def make_gain(j):
+            nc.vector.tensor_scalar(out=gain[j][:], in0=inv[j][:], scalar1=us_sb[:, j : j + 1], scalar2=None, op0=ALU.mult)
+
+        def even_on_vector(j, cols):
+            nc.vector.tensor_scalar(
+                out=hid_rows[:, j, cols], in0=a_ps[j][:, cols], scalar1=inv[j][:], scalar2=us_sb[:, j : j + 1],
+                op0=ALU.mult, op1=ALU.mult,
+            )
+
+        def even_on_scalar(j, cols):
+            nc.scalar.activation(out=hid_rows[:, j, cols], in_=a_ps[j][:, cols], func=ACT.Copy, scale=gain[j][:])
+
+        def deal_wy(z):
+            nc.vector.tensor_copy(
+                out=wy_codes[z][:].rearrange("p j m -> p m j"), in_=wy_raw[:, z, :].rearrange("p (m j) -> p m j", j=PACK)
+            )
+
+        every = slice(0, T)
+        quarter = [slice(q * TQ, (q + 1) * TQ) for q in range(NQ)]
+
+        for j in range(PACK):
+            mean_abs(j)
+        deal_plane(wy_plane, wy_plane_raw)
+        deal_wy(0)
+        add_tenth(0)
+        deal_wy(1)
+        invert(0)
+        nc.vector.tensor_copy(
+            out=wb_codes[:].rearrange("p j (m b) -> p j m b", b=2),
+            in_=wb_raw[:].rearrange("p (m j b) -> p j m b", j=PACK, b=2),
+        )
+        add_tenth(1)
+        even_on_vector(0, every)
+        invert(1)
+        add_tenth(2)
+        even_on_vector(1, every)
+        invert(2)
+        deal_plane(wb_plane, wb_plane_raw)
+        make_gain(2)
+        add_tenth(3)
+        invert(3)
+        even_on_vector(3, quarter[0])
+        make_gain(3)
+        even_on_scalar(2, every)
+        for q in range(1, NQ):
+            even_on_scalar(3, quarter[q])
+
+        y_ps = [ps.tile([P, PACK, TQ], F32, name="y_ps_%d" % q) for q in range(NQ)]
+        for q in range(NQ):
+            for i in range(PACK):
+                for z in range(PASSES):
+                    nc.tensor.matmul_mx(
+                        out=y_ps[q][:, i, :],
+                        lhsT=wy_codes[z][:, i, :].bitcast(E4M3),
+                        lhsT_scale=wy_plane[:, z, i, :],
+                        rhs=x_codes[:, z, 2 * q * TQ : 2 * (q + 1) * TQ].bitcast(E2M1),
+                        rhs_scale=x_plane[:, z, quarter[q]],
+                        start=(i == 0 and z == 0),
+                        stop=False,
+                    )
+
+        hid_words = [sbuf("hid_words_%d" % q, [P, TQ, PACK], BF16) for q in range(NQ)]
+        hid_codes = [sbuf("hid_codes_%d" % q, [P, TQ], I32) for q in range(NQ)]
+        hid_plane = [sbuf("hid_plane_%d" % q, [P, TQ], U8) for q in range(NQ)]
+        y_sb = [sbuf("y_sb_%d" % q, [P, PACK, TQ], F32) for q in range(NQ)]
+        y_words = [sbuf("y_words_%d" % q, [P, TQ, PACK], BF16) for q in range(NQ)]
+        y_codes = sbuf("y_codes", [P, T], I32)
+        y_plane = sbuf("y_plane", [P, T], U8)
+
+        def interleave(words, rows):
+            nc.vector.tensor_copy(
+                out=words.rearrange("p (c e) j -> p c j e", e=RUN), in_=rows.rearrange("p j (c e) -> p c j e", e=RUN)
+            )
+
+        def quantize(codes, plane, words):
+            nc.vector.quantize_mx(out=codes.bitcast(E4M3), scales=plane, in_=words.rearrange("p t j -> p (t j)"))
+
+        def second_layer(q):
+            for i in range(PACK):
+                nc.tensor.matmul_mx(
+                    out=y_ps[q][:, i, :],
+                    lhsT=wb_codes[:, i, :].bitcast(E2M1),
+                    lhsT_scale=wb_plane[:, 0, i, :],
+                    rhs=hid_codes[q][:].bitcast(E4M3),
+                    rhs_scale=hid_plane[q][:],
+                    start=False,
+                    stop=(i == PACK - 1),
+                )
+
+        out_rows = out_0.rearrange("(p i) t -> p i t", i=PACK)
+        out_words = out_1[0].rearrange("p c r -> p (c r)").bitcast(I32)
+
+        interleave(hid_words[0][:], hid_rows[:, :, quarter[0]])
+        for q in range(NQ):
+            if q + 1 < NQ:
+                interleave(hid_words[q + 1][:], hid_rows[:, :, quarter[q + 1]])
+            quantize(hid_codes[q][:], hid_plane[q][:], hid_words[q][:])
+            second_layer(q)
+            nc.scalar.copy(out=y_sb[q][:], in_=y_ps[q][:])
+            queue = nc.scalar if q == NQ - 1 else nc.sync
+            queue.dma_start(out=out_rows[:, :, quarter[q]], in_=y_sb[q][:])
+
+        interleave(y_words[0][:], y_sb[0][:])
+        for q in range(NQ):
+            if q + 1 < NQ:
+                interleave(y_words[q + 1][:], y_sb[q + 1][:])
+            quantize(y_codes[:, quarter[q]], y_plane[:, quarter[q]], y_words[q][:])
+            if q == NQ - 2:
+                nc.sync.dma_start(out=out_words[:, : (NQ - 1) * TQ], in_=y_codes[:, : (NQ - 1) * TQ])
+        nc.sync.dma_start(out=out_words[:, quarter[NQ - 1]], in_=y_codes[:, quarter[NQ - 1]])
+        for q in range(QUADS):
+            queue = nc.sync if q < 2 else nc.scalar
+            queue.dma_start(
+                out=out_2[0, 4 * q : 4 * q + 4, :].bitcast(I32), in_=y_plane[32 * q : 32 * q + 4, :].bitcast(I32)
+            )

@@ -37,7 +37,7 @@ def tile_mix_hidden_evened_and_skip_pl_kernel(
 
         x_codes = sbuf("x_codes", [P, PASSES, 2 * T], U8)
         x_plane = sbuf("x_plane", [P, PASSES, T], U8)
-        wa_raw = sbuf("wa_raw", [P, PASSES, R], I32)
+        wa_raw = [sbuf("wa_raw_%d" % z, [P, R], I32) for z in range(PASSES)]
         wa_plane_raw = sbuf("wa_plane_raw", [P, PASSES, R], U8)
         wy_raw = sbuf("wy_raw", [P, PASSES, N], I32)
         wy_plane_raw = sbuf("wy_plane_raw", [P, PASSES, N], U8)
@@ -47,7 +47,7 @@ def tile_mix_hidden_evened_and_skip_pl_kernel(
         warm = sbuf("warm", [P, 1], F32)
         warm_out = sbuf("warm_out", [P, 1], F32)
 
-        wa_codes = [[sbuf("wa_codes_%d_%d" % (h, z), [P, 2, P], I32) for z in range(PASSES)] for h in range(2)]
+        wa_codes = [sbuf("wa_codes_%d" % z, [P, PACK, P], I32) for z in range(PASSES)]
         wa_plane = sbuf("wa_plane", [P, PASSES, PACK, P], U8)
         wy_codes = [sbuf("wy_codes_%d" % z, [P, PACK, P], I32) for z in range(PASSES)]
         wy_plane = sbuf("wy_plane", [P, PASSES, PACK, P], U8)
@@ -72,40 +72,36 @@ def tile_mix_hidden_evened_and_skip_pl_kernel(
         zero(wy_plane_raw)
         zero(wb_plane_raw)
 
-        load_scale_rows(nc.scalar, wa_plane_raw, wa_scales, 0)
-        load_scale_rows(nc.scalar, wa_plane_raw, wa_scales, 1)
-        nc.sync.dma_start(out=wa_raw[:], in_=wa_words.rearrange("z p c r -> p z (c r)").bitcast(I32))
+        wa_hbm = wa_words.rearrange("z p c r -> p z (c r)").bitcast(I32)
         nc.sync.dma_start(out=x_codes[:].bitcast(I32), in_=xt_words.rearrange("z p c -> p z c").bitcast(I32))
-        load_scale_rows(nc.scalar, wa_plane_raw, wa_scales, 2)
-        load_scale_rows(nc.scalar, wa_plane_raw, wa_scales, 3)
+        for q in range(QUADS):
+            load_scale_rows(nc.scalar, wa_plane_raw, wa_scales, q)
+        nc.scalar.activation(out=warm_out[:], in_=warm[:], func=ACT.Abs)
         load_scale_rows(nc.sync, x_plane, xt_scales, 0)
         load_scale_rows(nc.sync, x_plane, xt_scales, 1)
-        nc.scalar.activation(out=warm_out[:], in_=warm[:], func=ACT.Abs)
-        load_scale_rows(nc.scalar, x_plane, xt_scales, 2)
-        load_scale_rows(nc.scalar, x_plane, xt_scales, 3)
+        nc.sync.dma_start(out=wa_raw[0][:], in_=wa_hbm[:, 0, :])
+        load_scale_rows(nc.sync, x_plane, xt_scales, 2)
+        load_scale_rows(nc.sync, x_plane, xt_scales, 3)
+        nc.sync.dma_start(out=wa_raw[1][:], in_=wa_hbm[:, 1, :])
+        for q in range(QUADS):
+            load_scale_rows(nc.sync, wy_plane_raw, wy_scales, q)
         nc.sync.dma_start(out=wy_raw[:], in_=wy_words.rearrange("z p c r -> p z (c r)").bitcast(I32))
+        nc.sync.dma_start(out=us_sb[:], in_=us.rearrange("(p j) o -> p (j o)", j=PACK))
         nc.sync.dma_start(out=wb_raw[:].bitcast(I32), in_=wb_words[0].bitcast(I32))
-        load_scale_rows(nc.scalar, wy_plane_raw, wy_scales, 0)
-        load_scale_rows(nc.scalar, wy_plane_raw, wy_scales, 1)
-        load_scale_rows(nc.sync, wy_plane_raw, wy_scales, 2)
-        load_scale_rows(nc.sync, wy_plane_raw, wy_scales, 3)
-        nc.scalar.dma_start(out=us_sb[:], in_=us.rearrange("(p j) o -> p (j o)", j=PACK))
         for q in range(QUADS):
             load_scale_rows(nc.sync, wb_plane_raw, wb_scales, q)
 
         deal_plane(wa_plane, wa_plane_raw)
-        for h in range(2):
-            for z in range(PASSES):
-                nc.vector.tensor_copy(
-                    out=wa_codes[h][z][:].rearrange("p j m -> p m j"),
-                    in_=wa_raw[:, z, :].rearrange("p (m j) -> p m j", j=PACK)[:, :, 2 * h : 2 * h + 2],
-                )
+        for z in range(PASSES):
+            nc.vector.tensor_copy(
+                out=wa_codes[z][:].rearrange("p j m -> p m j"), in_=wa_raw[z][:].rearrange("p (m j) -> p m j", j=PACK)
+            )
         a_ps = [ps.tile([P, T], F32, name="a_ps_%d" % j) for j in range(PACK)]
-        for j in range(PACK):
-            for z in range(PASSES):
+        for j, z in [(0, 0), (1, 0), (0, 1), (1, 1), (2, 0), (2, 1), (3, 0), (3, 1)]:
+            if True:
                 nc.tensor.matmul_mx(
                     out=a_ps[j][:],
-                    lhsT=wa_codes[j // 2][z][:, j % 2, :].bitcast(E4M3),
+                    lhsT=wa_codes[z][:, j, :].bitcast(E4M3),
                     lhsT_scale=wa_plane[:, z, j, :],
                     rhs=x_codes[:, z, :].bitcast(E2M1),
                     rhs_scale=x_plane[:, z, :],
@@ -146,6 +142,18 @@ def tile_mix_hidden_evened_and_skip_pl_kernel(
                 out=wy_codes[z][:].rearrange("p j m -> p m j"), in_=wy_raw[:, z, :].rearrange("p (m j) -> p m j", j=PACK)
             )
 
+        def deal_wb():
+            nc.vector.tensor_copy(
+                out=wb_codes[:].rearrange("p j (m b) -> p j m b", b=2),
+                in_=wb_raw[:].rearrange("p (m j b) -> p j m b", j=PACK, b=2),
+            )
+
+        def deal_wb_plane(h):
+            nc.vector.tensor_copy(
+                out=wb_plane[:, 0, 2 * h : 2 * h + 2, :],
+                in_=wb_plane_raw[:, 0, :].rearrange("p (m j) -> p j m", j=PACK)[:, 2 * h : 2 * h + 2, :],
+            )
+
         every = slice(0, T)
         quarter = [slice(q * TQ, (q + 1) * TQ) for q in range(NQ)]
 
@@ -153,28 +161,27 @@ def tile_mix_hidden_evened_and_skip_pl_kernel(
             mean_abs(j)
         deal_plane(wy_plane, wy_plane_raw)
         deal_wy(0)
-        add_tenth(0)
         deal_wy(1)
+        add_tenth(0)
+        deal_wb()
         invert(0)
-        nc.vector.tensor_copy(
-            out=wb_codes[:].rearrange("p j (m b) -> p j m b", b=2),
-            in_=wb_raw[:].rearrange("p (m j b) -> p j m b", j=PACK, b=2),
-        )
         add_tenth(1)
         even_on_vector(0, every)
         invert(1)
         add_tenth(2)
-        even_on_vector(1, every)
+        deal_wb_plane(0)
+        make_gain(1)
         invert(2)
-        deal_plane(wb_plane, wb_plane_raw)
-        make_gain(2)
         add_tenth(3)
+        make_gain(2)
         invert(3)
+        deal_wb_plane(1)
         even_on_vector(3, quarter[0])
         make_gain(3)
-        even_on_scalar(2, every)
-        for q in range(1, NQ):
-            even_on_scalar(3, quarter[q])
+        for q in range(NQ):
+            for j in range(1, PACK):
+                if q > 0 or j < PACK - 1:
+                    even_on_scalar(j, quarter[q])
 
         y_ps = [ps.tile([P, PACK, TQ], F32, name="y_ps_%d" % q) for q in range(NQ)]
         for q in range(NQ):
@@ -193,7 +200,7 @@ def tile_mix_hidden_evened_and_skip_pl_kernel(
         hid_words = [sbuf("hid_words_%d" % q, [P, TQ, PACK], BF16) for q in range(NQ)]
         hid_codes = [sbuf("hid_codes_%d" % q, [P, TQ], I32) for q in range(NQ)]
         hid_plane = [sbuf("hid_plane_%d" % q, [P, TQ], U8) for q in range(NQ)]
-        y_sb = [sbuf("y_sb_%d" % q, [P, PACK, TQ], F32) for q in range(NQ)]
+        y_sb = sbuf("y_sb", [P, PACK, T], F32)
         y_words = [sbuf("y_words_%d" % q, [P, TQ, PACK], BF16) for q in range(NQ)]
         y_codes = sbuf("y_codes", [P, T], I32)
         y_plane = sbuf("y_plane", [P, T], U8)
@@ -227,18 +234,16 @@ def tile_mix_hidden_evened_and_skip_pl_kernel(
                 interleave(hid_words[q + 1][:], hid_rows[:, :, quarter[q + 1]])
             quantize(hid_codes[q][:], hid_plane[q][:], hid_words[q][:])
             second_layer(q)
-            nc.scalar.copy(out=y_sb[q][:], in_=y_ps[q][:])
-            queue = nc.scalar if q == NQ - 1 else nc.sync
-            queue.dma_start(out=out_rows[:, :, quarter[q]], in_=y_sb[q][:])
+        for q, rows in [(0, slice(0, 2)), (0, slice(2, 4)), (1, slice(0, 4)), (2, slice(0, 4)), (3, slice(0, 4))]:
+            nc.scalar.copy(out=y_sb[:, rows, quarter[q]], in_=y_ps[q][:, rows, :])
+            nc.sync.dma_start(out=out_rows[:, rows, quarter[q]], in_=y_sb[:, rows, quarter[q]])
+        interleave(y_words[0][:], y_sb[:, :, quarter[0]])
 
-        interleave(y_words[0][:], y_sb[0][:])
         for q in range(NQ):
             if q + 1 < NQ:
-                interleave(y_words[q + 1][:], y_sb[q + 1][:])
+                interleave(y_words[q + 1][:], y_sb[:, :, quarter[q + 1]])
             quantize(y_codes[:, quarter[q]], y_plane[:, quarter[q]], y_words[q][:])
-            if q == NQ - 2:
-                nc.sync.dma_start(out=out_words[:, : (NQ - 1) * TQ], in_=y_codes[:, : (NQ - 1) * TQ])
-        nc.sync.dma_start(out=out_words[:, quarter[NQ - 1]], in_=y_codes[:, quarter[NQ - 1]])
+        nc.sync.dma_start(out=out_words, in_=y_codes[:])
         for q in range(QUADS):
             queue = nc.sync if q < 2 else nc.scalar
             queue.dma_start(

from contextlib import ExitStack

import concourse.mybir as mybir

K, T, R, N = 1024, 512, 512, 512
FLOPS = 2 * T * (K * R + R * N + K * N)

F32 = mybir.dt.float32
BF16 = mybir.dt.bfloat16
I32 = mybir.dt.int32
U8 = mybir.dt.uint8
E4M3 = mybir.dt.float8_e4m3fn_x4
E2M1 = mybir.dt.float4_e2m1fn_x4
ALU = mybir.AluOpType
ACT = mybir.ActivationFunctionType

P = 128
PACK = 4
PASSES = K // (P * PACK)
QUADS = 4
TQ = 128
NQ = T // TQ
RUN = 4


def tile_mix_hidden_evened_and_skip_pl_kernel(
    tc, xt_words, xt_scales, wa_words, wa_scales, us, wb_words, wb_scales, wy_words, wy_scales, out_0, out_1, out_2
):
    nc = tc.nc
    with ExitStack() as ctx:
        sb = ctx.enter_context(tc.tile_pool(name="sb", bufs=1))
        ps = ctx.enter_context(tc.psum_pool(name="ps", bufs=1))
        ctx.enter_context(tc.manual_schedule())

        def sbuf(name, shape, dtype):
            return sb.tile(shape, dtype, name=name, align_bytes=64)

        x_codes = sbuf("x_codes", [P, PASSES, 2 * T], U8)
        x_plane = sbuf("x_plane", [P, PASSES, T], U8)
        wa_raw = [sbuf("wa_raw_%d" % z, [P, R], I32) for z in range(PASSES)]
        wa_plane_raw = sbuf("wa_plane_raw", [P, PASSES, R], U8)
        wy_raw = sbuf("wy_raw", [P, PASSES, N], I32)
        wy_plane_raw = sbuf("wy_plane_raw", [P, PASSES, N], U8)
        wb_raw = sbuf("wb_raw", [P, 2 * N], U8)
        wb_plane_raw = sbuf("wb_plane_raw", [P, 1, N], U8)
        us_sb = sbuf("us_sb", [P, PACK], F32)
        warm = sbuf("warm", [P, 1], F32)
        warm_out = sbuf("warm_out", [P, 1], F32)

        wa_codes = [sbuf("wa_codes_%d" % z, [P, PACK, P], I32) for z in range(PASSES)]
        wa_plane = sbuf("wa_plane", [P, PASSES, PACK, P], U8)
        wy_codes = [sbuf("wy_codes_%d" % z, [P, PACK, P], I32) for z in range(PASSES)]
        wy_plane = sbuf("wy_plane", [P, PASSES, PACK, P], U8)
        wb_codes = sbuf("wb_codes", [P, PACK, 2 * P], U8)
        wb_plane = sbuf("wb_plane", [P, 1, PACK, P], U8)

        def load_scale_rows(queue, plane, scales, q):
            queue.dma_start(
                out=plane[32 * q : 32 * q + 4, :, :].bitcast(I32),
                in_=scales[:, 4 * q : 4 * q + 4, :].rearrange("z r c -> r z c").bitcast(I32),
            )

        def zero(plane):
            nc.vector.memset(plane[:].rearrange("p z c -> p (z c)").bitcast(I32), 0)

        def deal_plane(dealt, raw):
            nc.vector.tensor_copy(out=dealt[:], in_=raw[:].rearrange("p z (m j) -> p z j m", j=PACK))

        zero(wa_plane_raw)
        zero(x_plane)
        nc.vector.memset(warm[:], 0.0)
        zero(wy_plane_raw)
        zero(wb_plane_raw)

        wa_hbm = wa_words.rearrange("z p c r -> p z (c r)").bitcast(I32)
        nc.sync.dma_start(out=x_codes[:].bitcast(I32), in_=xt_words.rearrange("z p c -> p z c").bitcast(I32))
        for q in range(QUADS):
            load_scale_rows(nc.scalar, wa_plane_raw, wa_scales, q)
        nc.scalar.activation(out=warm_out[:], in_=warm[:], func=ACT.Abs)
        load_scale_rows(nc.sync, x_plane, xt_scales, 0)
        load_scale_rows(nc.sync, x_plane, xt_scales, 1)
        nc.sync.dma_start(out=wa_raw[0][:], in_=wa_hbm[:, 0, :])
        load_scale_rows(nc.sync, x_plane, xt_scales, 2)
        load_scale_rows(nc.sync, x_plane, xt_scales, 3)
        nc.sync.dma_start(out=wa_raw[1][:], in_=wa_hbm[:, 1, :])
        for q in range(QUADS):
            load_scale_rows(nc.sync, wy_plane_raw, wy_scales, q)
        nc.sync.dma_start(out=wy_raw[:], in_=wy_words.rearrange("z p c r -> p z (c r)").bitcast(I32))
        nc.sync.dma_start(out=us_sb[:], in_=us.rearrange("(p j) o -> p (j o)", j=PACK))
        nc.sync.dma_start(out=wb_raw[:].bitcast(I32), in_=wb_words[0].bitcast(I32))
        for q in range(QUADS):
            load_scale_rows(nc.sync, wb_plane_raw, wb_scales, q)

        deal_plane(wa_plane, wa_plane_raw)
        for z in range(PASSES):
            nc.vector.tensor_copy(
                out=wa_codes[z][:].rearrange("p j m -> p m j"), in_=wa_raw[z][:].rearrange("p (m j) -> p m j", j=PACK)
            )
        a_ps = [ps.tile([P, T], F32, name="a_ps_%d" % j) for j in range(PACK)]
        for j, z in [(0, 0), (1, 0), (0, 1), (1, 1), (2, 0), (2, 1), (3, 0), (3, 1)]:
            if True:
                nc.tensor.matmul_mx(
                    out=a_ps[j][:],
                    lhsT=wa_codes[z][:, j, :].bitcast(E4M3),
                    lhsT_scale=wa_plane[:, z, j, :],
                    rhs=x_codes[:, z, :].bitcast(E2M1),
                    rhs_scale=x_plane[:, z, :],
                    start=(z == 0),
                    stop=(z == PASSES - 1),
                )

        abs_a = [sbuf("abs_a_%d" % j, [P, T], BF16) for j in range(PACK)]
        mean = [sbuf("mean_%d" % j, [P, 1], F32) for j in range(PACK)]
        denom = [sbuf("denom_%d" % j, [P, 1], F32) for j in range(PACK)]
        inv = [sbuf("inv_%d" % j, [P, 1], F32) for j in range(PACK)]
        gain = [sbuf("gain_%d" % j, [P, 1], F32) for j in range(PACK)]
        hid_rows = sbuf("hid_rows", [P, PACK, T], BF16)

        def mean_abs(j):
            nc.scalar.activation(out=abs_a[j][:], in_=a_ps[j][:], func=ACT.Abs, scale=1.0 / T, accum_out=mean[j][:])

        def add_tenth(j):
            nc.vector.tensor_scalar(out=denom[j][:], in0=mean[j][:], scalar1=0.1, scalar2=None, op0=ALU.add)

        def invert(j):
            nc.vector.reciprocal(out=inv[j][:], in_=denom[j][:])

        def make_gain(j):
            nc.vector.tensor_scalar(out=gain[j][:], in0=inv[j][:], scalar1=us_sb[:, j : j + 1], scalar2=None, op0=ALU.mult)

        def even_on_vector(j, cols):
            nc.vector.tensor_scalar(
                out=hid_rows[:, j, cols], in0=a_ps[j][:, cols], scalar1=inv[j][:], scalar2=us_sb[:, j : j + 1],
                op0=ALU.mult, op1=ALU.mult,
            )

        def even_on_scalar(j, cols):
            nc.scalar.activation(out=hid_rows[:, j, cols], in_=a_ps[j][:, cols], func=ACT.Copy, scale=gain[j][:])

        def deal_wy(z):
            nc.vector.tensor_copy(
                out=wy_codes[z][:].rearrange("p j m -> p m j"), in_=wy_raw[:, z, :].rearrange("p (m j) -> p m j", j=PACK)
            )

        def deal_wb():
            nc.vector.tensor_copy(
                out=wb_codes[:].rearrange("p j (m b) -> p j m b", b=2),
                in_=wb_raw[:].rearrange("p (m j b) -> p j m b", j=PACK, b=2),
            )

        def deal_wb_plane(h):
            nc.vector.tensor_copy(
                out=wb_plane[:, 0, 2 * h : 2 * h + 2, :],
                in_=wb_plane_raw[:, 0, :].rearrange("p (m j) -> p j m", j=PACK)[:, 2 * h : 2 * h + 2, :],
            )

        every = slice(0, T)
        quarter = [slice(q * TQ, (q + 1) * TQ) for q in range(NQ)]

        for j in range(PACK):
            mean_abs(j)
        deal_plane(wy_plane, wy_plane_raw)
        deal_wy(0)
        deal_wy(1)
        add_tenth(0)
        deal_wb()
        invert(0)
        add_tenth(1)
        even_on_vector(0, every)
        invert(1)
        add_tenth(2)
        deal_wb_plane(0)
        make_gain(1)
        invert(2)
        add_tenth(3)
        make_gain(2)
        invert(3)
        deal_wb_plane(1)
        even_on_vector(3, quarter[0])
        make_gain(3)
        for q in range(NQ):
            for j in range(1, PACK):
                if q > 0 or j < PACK - 1:
                    even_on_scalar(j, quarter[q])

        y_ps = [ps.tile([P, PACK, TQ], F32, name="y_ps_%d" % q) for q in range(NQ)]
        for q in range(NQ):
            for i in range(PACK):
                for z in range(PASSES):
                    nc.tensor.matmul_mx(
                        out=y_ps[q][:, i, :],
                        lhsT=wy_codes[z][:, i, :].bitcast(E4M3),
                        lhsT_scale=wy_plane[:, z, i, :],
                        rhs=x_codes[:, z, 2 * q * TQ : 2 * (q + 1) * TQ].bitcast(E2M1),
                        rhs_scale=x_plane[:, z, quarter[q]],
                        start=(i == 0 and z == 0),
                        stop=False,
                    )

        hid_words = [sbuf("hid_words_%d" % q, [P, TQ, PACK], BF16) for q in range(NQ)]
        hid_codes = [sbuf("hid_codes_%d" % q, [P, TQ], I32) for q in range(NQ)]
        hid_plane = [sbuf("hid_plane_%d" % q, [P, TQ], U8) for q in range(NQ)]
        y_sb = sbuf("y_sb", [P, PACK, T], F32)
        y_words = [sbuf("y_words_%d" % q, [P, TQ, PACK], BF16) for q in range(NQ)]
        y_codes = sbuf("y_codes", [P, T], I32)
        y_plane = sbuf("y_plane", [P, T], U8)

        def interleave(words, rows):
            nc.vector.tensor_copy(
                out=words.rearrange("p (c e) j -> p c j e", e=RUN), in_=rows.rearrange("p j (c e) -> p c j e", e=RUN)
            )

        def quantize(codes, plane, words):
            nc.vector.quantize_mx(out=codes.bitcast(E4M3), scales=plane, in_=words.rearrange("p t j -> p (t j)"))

        def second_layer(q):
            for i in range(PACK):
                nc.tensor.matmul_mx(
                    out=y_ps[q][:, i, :],
                    lhsT=wb_codes[:, i, :].bitcast(E2M1),
                    lhsT_scale=wb_plane[:, 0, i, :],
                    rhs=hid_codes[q][:].bitcast(E4M3),
                    rhs_scale=hid_plane[q][:],
                    start=False,
                    stop=(i == PACK - 1),
                )

        out_rows = out_0.rearrange("(p i) t -> p i t", i=PACK)
        out_words = out_1[0].rearrange("p c r -> p (c r)").bitcast(I32)

        interleave(hid_words[0][:], hid_rows[:, :, quarter[0]])
        for q in range(NQ):
            if q + 1 < NQ:
                interleave(hid_words[q + 1][:], hid_rows[:, :, quarter[q + 1]])
            quantize(hid_codes[q][:], hid_plane[q][:], hid_words[q][:])
            second_layer(q)
        for q, rows in [(0, slice(0, 2)), (0, slice(2, 4)), (1, slice(0, 4)), (2, slice(0, 4)), (3, slice(0, 4))]:
            nc.scalar.copy(out=y_sb[:, rows, quarter[q]], in_=y_ps[q][:, rows, :])
            nc.sync.dma_start(out=out_rows[:, rows, quarter[q]], in_=y_sb[:, rows, quarter[q]])
        interleave(y_words[0][:], y_sb[:, :, quarter[0]])

        for q in range(NQ):
            if q + 1 < NQ:
                interleave(y_words[q + 1][:], y_sb[:, :, quarter[q + 1]])
            quantize(y_codes[:, quarter[q]], y_plane[:, quarter[q]], y_words[q][:])
        nc.sync.dma_start(out=out_words, in_=y_codes[:])
        for q in range(QUADS):
            queue = nc.sync if q < 2 else nc.scalar
            queue.dma_start(
                out=out_2[0, 4 * q : 4 * q + 4, :].bitcast(I32), in_=y_plane[32 * q : 32 * q + 4, :].bitcast(I32)
            )
